import numpy as np
import ml_dtypes


def mxq(x, axis, fmt="e4m3"):
    dtype, down = {"e4m3": (ml_dtypes.float8_e4m3fn, 7), "e5m2": (ml_dtypes.float8_e5m2, 14)}[fmt]
    v = np.moveaxis(np.asarray(x, np.float32).astype(ml_dtypes.bfloat16).astype(np.float64), axis, -1)
    blocks = v.reshape(v.shape[:-1] + (-1, 32))
    amax = np.abs(blocks).max(-1, keepdims=True)
    byte = np.maximum(np.where(amax > 0, np.frexp(amax)[1] - 1 + 127, 0) - down, 1)
    scale = np.exp2(byte - 127.0)
    codes = (blocks / scale).astype(np.float32).astype(dtype).astype(np.float64)
    return np.moveaxis((codes * scale).reshape(v.shape), -1, axis)


WIDE = False


def mx_kscale(k):
    if not WIDE:
        return np.ones(k)
    levels = np.array([30, -30])
    if k % 512:
        return np.exp2(np.random.permutation(np.resize(levels, k // 32))).repeat(32)
    a = np.empty((k // 512, 16))
    for p in range(k // 512):
        a[p, :8] = np.random.permutation(np.resize(levels, 8))
        for g in range(8):
            far = levels[np.abs(levels - a[p, g]) >= 10]
            a[p, g + 8] = far[np.random.randint(len(far))]
    return np.exp2(a.ravel()).repeat(32)


def f64(x):
    return np.asarray(x).astype(np.float64)


def striped(idx):
    return np.tile(np.asarray(idx).reshape(-1, 16).T, (8, 1)).astype(np.uint16)


def unstriped(offs):
    return offs[:16].T.reshape(-1).astype(np.int64)


def striped8(idx):
    return np.asarray(idx).reshape(8, -1, 16).transpose(0, 2, 1).reshape(128, -1).astype(np.uint16)


def unstriped8(offs):
    return offs.reshape(8, 16, -1).transpose(0, 2, 1).reshape(8, -1).astype(np.int64)


def pick8(x, idx, run):
    r = np.arange(len(x))
    return x[r[:, None], idx[r % (8 * run) // run]]


E2M1 = np.array([0.0, 0.5, 1.0, 1.5, 2.0, 3.0, 4.0, 6.0, -0.0, -0.5, -1.0, -1.5, -2.0, -3.0, -4.0, -6.0])


def pack_weight(w, fmt):
    k, n = w.shape
    w = f64(np.asarray(w, np.float32).astype(ml_dtypes.bfloat16)).reshape(k // 32, 32, n)
    amax = np.abs(w).max(1)
    if fmt in ("e4m3", "e5m2"):
        byte = np.frexp(amax)[1] - 1 + 127 - (7 if fmt == "e4m3" else 14)
    else:
        mant, ex = np.frexp(amax / 6.0)
        byte = np.where(mant > 0.5, ex, ex - 1) + 127
    byte = np.clip(np.where(amax > 0, byte, 1), 1, 254)
    scaled = (w * np.exp2(127.0 - byte)[:, None, :]).reshape(k, n).astype(np.float32)
    by_word = np.ascontiguousarray(scaled.reshape(k // 512, 128, 4, n).transpose(0, 1, 3, 2))
    if fmt in ("e4m3", "e5m2"):
        words = by_word.astype(ml_dtypes.float8_e4m3fn if fmt == "e4m3" else ml_dtypes.float8_e5m2).view(np.uint8)
    else:
        c = by_word.astype(ml_dtypes.float4_e2m1fn).view(np.uint8) & 0xF
        words = (c[..., 0::2] | (c[..., 1::2] << 4)).reshape(k // 512, 128, 2 * n)
    return np.ascontiguousarray(words), np.ascontiguousarray(byte.astype(np.uint8).reshape(k // 512, 16, n))


def unpack_weight(words, scales, fmt):
    g, _, n = scales.shape
    words = np.ascontiguousarray(words).reshape(g, 128, n, -1)
    if fmt in ("e4m3", "e5m2"):
        vals = words.view(ml_dtypes.float8_e4m3fn if fmt == "e4m3" else ml_dtypes.float8_e5m2).astype(np.float64)
    else:
        nib = np.empty((g, 128, n, 4), np.uint8)
        nib[..., 0::2] = words & 0xF
        nib[..., 1::2] = words >> 4
        vals = E2M1[nib]
    vals = vals * np.repeat(np.exp2(scales.astype(np.float64) - 127.0), 8, axis=1)[..., None]
    return vals.transpose(0, 1, 3, 2).reshape(g * 512, n)


K, T, Z, J, R, C, O, N = 512, 1024, 1024, 256, 512, 512, 128, 256


def setup_inputs():
    n = np.random.standard_normal
    idx = np.random.permutation(T)[:J]
    idx2 = np.random.permutation(Z)[:J]
    idx3 = np.stack([np.random.permutation(C)[:J] for _ in range(8)])
    idx4 = np.stack([np.random.permutation(C)[:O] for _ in range(8)])
    idx5 = np.random.permutation(J)[:O]
    fk = mx_kscale(K)
    fr = mx_kscale(R)
    xtp = pack_weight(n((K, T)) / fk[:, None], "e5m2")
    xop = pack_weight(n((K, Z)) / fk[:, None], "e4m3")
    wp = pack_weight(n((K, R)) * 1 / np.sqrt(K) * fk[:, None] * fr, "e2m1")
    w2p = pack_weight(n((K, R)) * 1 / np.sqrt(K) * fk[:, None] * fr, "e5m2")
    wbp = pack_weight(n((R, N)) * 1 / np.sqrt(R) / fr[:, None], "e2m1")
    return {
        "xt_words": xtp[0],
        "xt_scales": xtp[1],
        "xo_words": xop[0],
        "xo_scales": xop[1],
        "w_words": wp[0],
        "w_scales": wp[1],
        "w2_words": w2p[0],
        "w2_scales": w2p[1],
        "sa": (np.random.uniform(0.5, 1.6, (R, 1))).astype(np.float32),
        "wb_words": wbp[0],
        "wb_scales": wbp[1],
        "offs": striped(idx),
        "offs2": striped(idx2),
        "offs3": striped8(idx3),
        "offs4": striped8(idx4),
        "offs5": striped(idx5),
    }


def reference(xt_words, xt_scales, xo_words, xo_scales, w_words, w_scales, w2_words, w2_scales, sa, wb_words, wb_scales, offs, offs2, offs3, offs4, offs5):
    idx = unstriped(offs)
    idx2 = unstriped(offs2)
    idx3 = unstriped8(offs3)
    idx4 = unstriped8(offs4)
    idx5 = unstriped(offs5)
    xtu = unpack_weight(xt_words, xt_scales, "e5m2")
    xou = unpack_weight(xo_words, xo_scales, "e4m3")
    wu = unpack_weight(w_words, w_scales, "e2m1")
    w2u = unpack_weight(w2_words, w2_scales, "e5m2")
    wbu = unpack_weight(wb_words, wb_scales, "e2m1")
    xtidxg = xtu[:, idx]
    xoidx2g = xou[:, idx2]
    a = wu.T @ xtidxg + w2u.T @ xoidx2g
    b = w2u.T @ xtidxg + wu.T @ xoidx2g
    pw = np.zeros((R, C))
    pw[np.arange(R)[:, None], idx3[np.arange(R) % 512 // 64]] = a
    hid = np.abs(pick8(pw, idx4, 64) * f64(sa) - b[:, idx5])
    hidq = mxq(hid, 0, "e4m3")
    y = wbu.T @ hidq
    return y

@@ -1,0 +1,173 @@
+from contextlib import ExitStack
+
+import concourse.mybir as mybir
+
+K, T, J, R, C, O, N = 512, 1024, 256, 512, 512, 128, 256
+FLOPS = 570425344
+
+F32 = mybir.dt.float32
+BF16 = mybir.dt.bfloat16
+I32 = mybir.dt.int32
+U32 = mybir.dt.uint32
+U16 = mybir.dt.uint16
+U8 = mybir.dt.uint8
+E4M3 = mybir.dt.float8_e4m3fn_x4
+E5M2 = mybir.dt.float8_e5m2_x4
+E2M1 = mybir.dt.float4_e2m1fn_x4
+ACT = mybir.ActivationFunctionType
+ALU = mybir.AluOpType
+
+P = 128
+PACK = 4
+H = J // 2
+SPLIT = 96
+
+
+def tile_list_groupboard_crossed_one_plain_kernel(
+    tc, xt_words, xt_scales, xo_words, xo_scales, w_words, w_scales, w2_words, w2_scales,
+    sa, wb_words, wb_scales, offs, offs2, offs3, offs4, offs5, out,
+):
+    nc = tc.nc
+    with ExitStack() as ctx:
+        sb = ctx.enter_context(tc.tile_pool(name="sb", bufs=1))
+        ps = ctx.enter_context(tc.psum_pool(name="ps", bufs=1))
+
+        def tile(name, shape, dtype):
+            return sb.tile(shape, dtype, name=name, align_bytes=64)
+
+        l1 = tile("l1", [P, J // 16], U16)
+        l2 = tile("l2", [P, J // 16], U16)
+        l3 = tile("l3", [P, J // 16], U16)
+        l4 = tile("l4", [P, O // 16], U16)
+        l5 = tile("l5", [P, O // 16], U16)
+
+        wsc = tile("wsc", [P, 2, 2, R // 4], I32)
+        xt_stage = tile("xt_stage", [P, 2, T // 4], I32)
+        xo_stage = tile("xo_stage", [P, 2, T // 4], I32)
+        xts = tile("xts", [P, T], U8)
+        xos = tile("xos", [P, T], U8)
+        xtw = tile("xtw", [P, T], I32)
+        xow = tile("xow", [P, T], I32)
+        w_raw = tile("w_raw", [P, R // 2], I32)
+        w2_raw = tile("w2_raw", [P, R], I32)
+        wb_w = tile("wb_w", [P, 2 * N], U8)
+        wb_s = tile("wb_s", [P, N], U8)
+        sa_t = tile("sa_t", [P, PACK], F32)
+
+        def quadrant_pairs(scales):
+            return scales[0].bitcast(I32).rearrange("(h u r) n -> u r h n", h=2, u=2)
+
+        nc.sync.dma_start(l1[:], offs)
+        nc.sync.dma_start(l2[:], offs2)
+        nc.vector.memset(xt_stage[0:64], 0)
+        nc.vector.memset(xo_stage[64:128], 0)
+        nc.vector.memset(wsc[:], 0)
+        for stage, base, src, q in ((xt_stage, 0, xt_scales, nc.sync), (xo_stage, 64, xo_scales, nc.scalar)):
+            for u in range(2):
+                q.dma_start(stage[base + 32 * u : base + 32 * u + 4], quadrant_pairs(src)[u])
+        nc.sync.dma_start(xtw[:], xt_words[0].rearrange("p n t -> p (n t)").bitcast(I32))
+        nc.sync.dma_start(xow[:], xo_words[0].rearrange("p n t -> p (n t)").bitcast(I32))
+        nc.sync.dma_start(w_raw[:], w_words[0].bitcast(I32))
+        nc.sync.dma_start(w2_raw[:], w2_words[0].rearrange("p n t -> p (n t)").bitcast(I32))
+        for s, src in enumerate((w_scales, w2_scales)):
+            for u in range(2):
+                nc.scalar.dma_start(wsc[32 * u : 32 * u + 4, :, s, :], quadrant_pairs(src)[u])
+        nc.sync.dma_start(l3[:], offs3)
+        nc.sync.dma_start(l5[:], offs5)
+        nc.sync.dma_start(l4[:], offs4)
+        nc.sync.dma_start(sa_t[:], sa.rearrange("(p i) one -> p (i one)", i=PACK))
+        nc.sync.dma_start(wb_w[:].bitcast(I32), wb_words[0].bitcast(I32))
+
+        boards = [tile(f"board{i}", [P, C], F32) for i in range(PACK)]
+        for board in boards:
+            nc.vector.memset(board[:], 0.0)
+        nc.vector.memset(wb_s[:].bitcast(I32), 0)
+        for q in range(4):
+            nc.sync.dma_start(wb_s[32 * q : 32 * q + 4].bitcast(I32), wb_scales[0, 4 * q : 4 * q + 4].bitcast(I32))
+
+        for plane, stage, base, order in ((xts, xt_stage, 0, (0, 1)), (xos, xo_stage, 64, (1, 0))):
+            for h in order:
+                nc.vector.tensor_copy(plane[64 * h : 64 * h + 64].bitcast(I32), stage[base : base + 64, h])
+
+        xtg = tile("xtg", [P, J], U32)
+        xog = tile("xog", [P, J], U32)
+        xtsg = tile("xtsg", [P, J], U8)
+        xosg = tile("xosg", [P, J], U8)
+        nc.vector.tensor_copy(xtsg[:], xts[:].indirect(l1[:]))
+        nc.vector.tensor_copy(xtg[:], xtw[:].bitcast(U32).indirect(l1[:]))
+
+        nc.vector.tensor_copy(wsc[64:128, 0], wsc[0:64, 1])
+        ws = tile("ws", [P, PACK, 2, P], U8)
+        ws_src = wsc[:, 0].bitcast(U8).rearrange("p s (m i) -> p i s m", i=PACK)
+        nc.vector.tensor_copy(ws[:, 0], ws_src[:, 0])
+
+        halves = [(slice(H * h, H * (h + 1)), slice(H // 16 * h, H // 16 * (h + 1))) for h in range(2)]
+        for js, ls in halves:
+            nc.vector.tensor_copy(xosg[:, js], xos[:].indirect(l2[:, ls]))
+            nc.vector.tensor_copy(xog[:, js], xow[:].bitcast(U32).indirect(l2[:, ls]))
+        nc.vector.tensor_copy(ws[:, 1:], ws_src[:, 1:])
+
+        w_p = tile("w_p", [P, PACK, 2 * P], U8)
+        w2_p = tile("w2_p", [P, PACK, P], U32)
+        w_src = w_raw[:].bitcast(U16).rearrange("p (m i) -> p m i", i=PACK)
+        w2_src = w2_raw[:].bitcast(U32).rearrange("p (m i) -> p m i", i=PACK)
+        nc.scalar.copy(w_p[:].bitcast(U16).rearrange("p i m -> p m i"), w_src)
+        nc.scalar.copy(w2_p[:, 0, :], w2_src[:, :, 0])
+        nc.scalar.copy(w2_p[:, 1:].rearrange("p i m -> p m i"), w2_src[:, :, 1:])
+
+        def product(acc, i, first, js):
+            lhs = (w_p[:, i, :].bitcast(E2M1), w2_p[:, i, :].bitcast(E5M2))
+            nc.tensor.matmul_mx(out=acc, lhsT=lhs[first], lhsT_scale=ws[:, i, first, :],
+                                rhs=xtg[:, js].bitcast(E5M2), rhs_scale=xtsg[:, js], start=True, stop=False)
+            nc.tensor.matmul_mx(out=acc, lhsT=lhs[1 - first], lhsT_scale=ws[:, i, 1 - first, :],
+                                rhs=xog[:, js].bitcast(E4M3), rhs_scale=xosg[:, js], start=False, stop=True)
+
+        a_sb = tile("a_sb", [P, PACK, J], F32)
+        b_sb = [tile(f"b_sb{i}", [P, J], F32) for i in range(PACK)]
+        picked = tile("picked", [P, PACK, O], F32)
+        beside = tile("beside", [P, PACK, O], F32)
+        diff = tile("diff", [P, PACK, O], F32)
+
+        for h, (js, ls) in enumerate(halves):
+            acc = ps.tile([P, H], F32, name=f"a0_ps{h}", tag=f"bank{h}")
+            product(acc[:], 0, 0, js)
+            nc.scalar.copy(a_sb[:, 0, js], acc[:])
+            nc.vector.tensor_copy(boards[0][:].indirect(l3[:, ls]), a_sb[:, 0, js])
+        for i in range(1, PACK):
+            acc = ps.tile([P, J], F32, name=f"a_ps{i}")
+            product(acc[:], i, 0, slice(0, J))
+            nc.scalar.copy(a_sb[:, i, :], acc[:])
+            nc.vector.tensor_copy(boards[i][:].indirect(l3[:]), a_sb[:, i, :])
+        b_ps = [ps.tile([P, 2, J], F32, name=f"b_ps{i}") for i in range(PACK // 2)]
+        for i in range(PACK):
+            product(b_ps[i // 2][:, i % 2, :], i, 1, slice(0, J))
+        for i in range(PACK):
+            nc.scalar.copy(b_sb[i][:], b_ps[i // 2][:, i % 2, :])
+            nc.scalar.activation(beside[:, i, :], b_sb[i][:].indirect(l5[:]), ACT.Copy)
+        for i in range(PACK):
+            nc.scalar.activation(picked[:, i, :], boards[i][:].indirect(l4[:]), ACT.Copy, scale=sa_t[:, i : i + 1])
+        nc.vector.tensor_tensor(diff[:, :3], picked[:, :3], beside[:, :3], ALU.subtract)
+        nc.vector.tensor_tensor(diff[:, 3], picked[:, 3], beside[:, 3], ALU.subtract)
+
+        hid = tile("hid", [P, O * PACK], BF16)
+        hid_v = hid[:].rearrange("p (o i) -> p o i", i=PACK)
+        diff_v = diff[:].rearrange("p i o -> p o i")
+        nc.scalar.activation(hid[:, : PACK * SPLIT].rearrange("p (c e i) -> p c i e", e=4, i=PACK),
+                             diff[:, :, :SPLIT].rearrange("p i (c e) -> p c i e", e=4), ACT.Abs)
+        nc.vector.scalar_tensor_tensor(hid_v[:, SPLIT:], diff_v[:, SPLIT:], -1.0, diff_v[:, SPLIT:], ALU.mult, ALU.max)
+        hq = tile("hq", [P, O], U32)
+        hs = tile("hs", [P, O], U8)
+        nc.vector.quantize_mx(out=hq[:].bitcast(E4M3), scales=hs[:], in_=hid[:])
+
+        for n in range(N // P):
+            y_ps = ps.tile([P, O], F32, name=f"y_ps{n}", tag=f"bank{n}")
+            nc.tensor.matmul_mx(out=y_ps[:], lhsT=wb_w[:, 2 * P * n : 2 * P * (n + 1)].bitcast(E2M1),
+                                lhsT_scale=wb_s[:, P * n : P * (n + 1)],
+                                rhs=hq[:].bitcast(E4M3), rhs_scale=hs[:], start=True, stop=True)
+            y = tile(f"y{n}", [P, O], F32)
+            if n == 0:
+                nc.vector.tensor_copy(y[:], y_ps[:])
+                nc.sync.dma_start(out[P * n : P * (n + 1), :], y[:])
+            else:
+                nc.scalar.copy(y[:], y_ps[:])
+                nc.scalar.dma_start(out[P * n : P * (n + 1), :], y[:])

@@ -32,8 +32,8 @@ def tile_list_groupboard_crossed_one_plain_kernel(
         sb = ctx.enter_context(tc.tile_pool(name="sb", bufs=1))
         ps = ctx.enter_context(tc.psum_pool(name="ps", bufs=1))
 
-        def tile(name, shape, dtype):
-            return sb.tile(shape, dtype, name=name, align_bytes=64)
+        def tile(name, shape, dtype, tag=""):
+            return sb.tile(shape, dtype, name=name, tag=tag or name, align_bytes=64)
 
         l1 = tile("l1", [P, J // 16], U16)
         l2 = tile("l2", [P, J // 16], U16)
@@ -58,34 +58,33 @@ def tile_list_groupboard_crossed_one_plain_kernel(
             return scales[0].bitcast(I32).rearrange("(h u r) n -> u r h n", h=2, u=2)
 
         nc.sync.dma_start(l1[:], offs)
-        nc.sync.dma_start(l2[:], offs2)
-        nc.vector.memset(xt_stage[0:64], 0)
-        nc.vector.memset(xo_stage[64:128], 0)
-        nc.vector.memset(wsc[:], 0)
-        for stage, base, src, q in ((xt_stage, 0, xt_scales, nc.sync), (xo_stage, 64, xo_scales, nc.scalar)):
-            for u in range(2):
-                q.dma_start(stage[base + 32 * u : base + 32 * u + 4], quadrant_pairs(src)[u])
-        nc.sync.dma_start(xtw[:], xt_words[0].rearrange("p n t -> p (n t)").bitcast(I32))
-        nc.sync.dma_start(xow[:], xo_words[0].rearrange("p n t -> p (n t)").bitcast(I32))
-        nc.sync.dma_start(w_raw[:], w_words[0].bitcast(I32))
+        nc.sync.dma_start(l3[:], offs3)
         nc.sync.dma_start(w2_raw[:], w2_words[0].rearrange("p n t -> p (n t)").bitcast(I32))
+        nc.vector.memset(xo_stage[64:128], 0)
+        nc.vector.memset(xt_stage[0:64], 0)
+        nc.vector.memset(wsc[:], 0)
+        for stage, base, src in ((xo_stage, 64, xo_scales), (xt_stage, 0, xt_scales)):
+            for u in range(2):
+                nc.sync.dma_start(stage[base + 32 * u : base + 32 * u + 4], quadrant_pairs(src)[u])
+        nc.sync.dma_start(xtw[:], xt_words[0].rearrange("p n t -> p (n t)").bitcast(I32))
         for s, src in enumerate((w_scales, w2_scales)):
             for u in range(2):
-                nc.scalar.dma_start(wsc[32 * u : 32 * u + 4, :, s, :], quadrant_pairs(src)[u])
-        nc.sync.dma_start(l3[:], offs3)
+                nc.sync.dma_start(wsc[32 * u : 32 * u + 4, :, s, :], quadrant_pairs(src)[u])
+        nc.sync.dma_start(xow[:], xo_words[0].rearrange("p n t -> p (n t)").bitcast(I32))
+        nc.sync.dma_start(l2[:], offs2)
+        nc.sync.dma_start(w_raw[:], w_words[0].bitcast(I32))
         nc.sync.dma_start(l5[:], offs5)
         nc.sync.dma_start(l4[:], offs4)
         nc.sync.dma_start(sa_t[:], sa.rearrange("(p i) one -> p (i one)", i=PACK))
         nc.sync.dma_start(wb_w[:].bitcast(I32), wb_words[0].bitcast(I32))
 
-        boards = [tile(f"board{i}", [P, C], F32) for i in range(PACK)]
-        for board in boards:
-            nc.vector.memset(board[:], 0.0)
+        boards = [tile("board0", [P, C], F32)]
+        nc.vector.memset(boards[0][:], 0.0)
         nc.vector.memset(wb_s[:].bitcast(I32), 0)
         for q in range(4):
             nc.sync.dma_start(wb_s[32 * q : 32 * q + 4].bitcast(I32), wb_scales[0, 4 * q : 4 * q + 4].bitcast(I32))
 
-        for plane, stage, base, order in ((xts, xt_stage, 0, (0, 1)), (xos, xo_stage, 64, (1, 0))):
+        for plane, stage, base, order in ((xos, xo_stage, 64, (1, 0)), (xts, xt_stage, 0, (0, 1))):
             for h in order:
                 nc.vector.tensor_copy(plane[64 * h : 64 * h + 64].bitcast(I32), stage[base : base + 64, h])
 
@@ -96,33 +95,38 @@ def tile_list_groupboard_crossed_one_plain_kernel(
         nc.vector.tensor_copy(xtsg[:], xts[:].indirect(l1[:]))
         nc.vector.tensor_copy(xtg[:], xtw[:].bitcast(U32).indirect(l1[:]))
 
-        nc.vector.tensor_copy(wsc[64:128, 0], wsc[0:64, 1])
-        ws = tile("ws", [P, PACK, 2, P], U8)
+        ws0 = tile("ws0", [P, 2, P], U8)
         ws_src = wsc[:, 0].bitcast(U8).rearrange("p s (m i) -> p i s m", i=PACK)
-        nc.vector.tensor_copy(ws[:, 0], ws_src[:, 0])
+        nc.vector.tensor_copy(wsc[64:128, 0], wsc[0:64, 1])
+        nc.vector.tensor_copy(ws0[:], ws_src[:, 0])
 
         halves = [(slice(H * h, H * (h + 1)), slice(H // 16 * h, H // 16 * (h + 1))) for h in range(2)]
-        for js, ls in halves:
+        for h, (js, ls) in enumerate(halves):
             nc.vector.tensor_copy(xosg[:, js], xos[:].indirect(l2[:, ls]))
             nc.vector.tensor_copy(xog[:, js], xow[:].bitcast(U32).indirect(l2[:, ls]))
-        nc.vector.tensor_copy(ws[:, 1:], ws_src[:, 1:])
+        ws1 = tile("ws1", [P, PACK - 1, 2, P], U8, "xos")
+        nc.vector.tensor_copy(ws1[:], ws_src[:, 1:])
+        ws = [ws0[:]] + [ws1[:, i] for i in range(PACK - 1)]
+        for i, tag in enumerate(("wsc", "xow")):
+            boards.append(tile(f"board{i + 1}", [P, C], F32, tag))
+            nc.gpsimd.memset(boards[-1][:], 0.0)
 
         w_p = tile("w_p", [P, PACK, 2 * P], U8)
         w2_p = tile("w2_p", [P, PACK, P], U32)
         w_src = w_raw[:].bitcast(U16).rearrange("p (m i) -> p m i", i=PACK)
         w2_src = w2_raw[:].bitcast(U32).rearrange("p (m i) -> p m i", i=PACK)
-        nc.scalar.copy(w_p[:].bitcast(U16).rearrange("p i m -> p m i"), w_src)
-        nc.scalar.copy(w2_p[:, 0, :], w2_src[:, :, 0])
-        nc.scalar.copy(w2_p[:, 1:].rearrange("p i m -> p m i"), w2_src[:, :, 1:])
+        nc.scalar.copy(w2_p[:].rearrange("p i m -> p m i"), w2_src)
+        nc.scalar.copy(w_p[:, 0, :].bitcast(U16), w_src[:, :, 0])
+        nc.scalar.copy(w_p[:, 1:].bitcast(U16).rearrange("p i m -> p m i"), w_src[:, :, 1:])
 
         def product(acc, i, first, js):
-            lhs = (w_p[:, i, :].bitcast(E2M1), w2_p[:, i, :].bitcast(E5M2))
-            nc.tensor.matmul_mx(out=acc, lhsT=lhs[first], lhsT_scale=ws[:, i, first, :],
-                                rhs=xtg[:, js].bitcast(E5M2), rhs_scale=xtsg[:, js], start=True, stop=False)
-            nc.tensor.matmul_mx(out=acc, lhsT=lhs[1 - first], lhsT_scale=ws[:, i, 1 - first, :],
-                                rhs=xog[:, js].bitcast(E4M3), rhs_scale=xosg[:, js], start=False, stop=True)
+            moving = ((xtg[:, js].bitcast(E5M2), xtsg[:, js]), (xog[:, js].bitcast(E4M3), xosg[:, js]))
+            for s, lhs in enumerate((w_p[:, i, :].bitcast(E2M1), w2_p[:, i, :].bitcast(E5M2))):
+                rhs, rhs_scale = moving[(first + s) % 2]
+                nc.tensor.matmul_mx(out=acc, lhsT=lhs, lhsT_scale=ws[i][:, s, :], rhs=rhs, rhs_scale=rhs_scale,
+                                    start=(s == 0), stop=(s == 1))
 
-        a_sb = tile("a_sb", [P, PACK, J], F32)
+        a_sb = [tile(f"a_sb{i}", [P, J], F32) for i in range(PACK)]
         b_sb = [tile(f"b_sb{i}", [P, J], F32) for i in range(PACK)]
         picked = tile("picked", [P, PACK, O], F32)
         beside = tile("beside", [P, PACK, O], F32)
@@ -131,13 +135,15 @@ def tile_list_groupboard_crossed_one_plain_kernel(
         for h, (js, ls) in enumerate(halves):
             acc = ps.tile([P, H], F32, name=f"a0_ps{h}", tag=f"bank{h}")
             product(acc[:], 0, 0, js)
-            nc.scalar.copy(a_sb[:, 0, js], acc[:])
-            nc.vector.tensor_copy(boards[0][:].indirect(l3[:, ls]), a_sb[:, 0, js])
+            nc.scalar.copy(a_sb[0][:, js], acc[:])
+            nc.vector.tensor_copy(boards[0][:].indirect(l3[:, ls]), a_sb[0][:, js])
+        boards.append(tile("board3", [P, C], F32, "a_sb0"))
+        nc.gpsimd.memset(boards[-1][:], 0.0)
         for i in range(1, PACK):
             acc = ps.tile([P, J], F32, name=f"a_ps{i}")
             product(acc[:], i, 0, slice(0, J))
-            nc.scalar.copy(a_sb[:, i, :], acc[:])
-            nc.vector.tensor_copy(boards[i][:].indirect(l3[:]), a_sb[:, i, :])
+            nc.scalar.copy(a_sb[i][:], acc[:])
+            nc.vector.tensor_copy(boards[i][:].indirect(l3[:]), a_sb[i][:])
         b_ps = [ps.tile([P, 2, J], F32, name=f"b_ps{i}") for i in range(PACK // 2)]
         for i in range(PACK):
             product(b_ps[i // 2][:, i % 2, :], i, 1, slice(0, J))

@@ -98,14 +98,14 @@ def tile_list_groupboard_crossed_one_plain_kernel(
         ws0 = tile("ws0", [P, 2, P], U8)
         ws_src = wsc[:, 0].bitcast(U8).rearrange("p s (m i) -> p i s m", i=PACK)
         nc.vector.tensor_copy(wsc[64:128, 0], wsc[0:64, 1])
-        nc.vector.tensor_copy(ws0[:], ws_src[:, 0])
+        nc.gpsimd.tensor_copy(ws0[:], ws_src[:, 0])
 
         halves = [(slice(H * h, H * (h + 1)), slice(H // 16 * h, H // 16 * (h + 1))) for h in range(2)]
         for h, (js, ls) in enumerate(halves):
             nc.vector.tensor_copy(xosg[:, js], xos[:].indirect(l2[:, ls]))
             nc.vector.tensor_copy(xog[:, js], xow[:].bitcast(U32).indirect(l2[:, ls]))
-        ws1 = tile("ws1", [P, PACK - 1, 2, P], U8, "xos")
-        nc.vector.tensor_copy(ws1[:], ws_src[:, 1:])
+        ws1 = tile("ws1", [P, PACK - 1, 2, P], U8)
+        nc.gpsimd.tensor_copy(ws1[:], ws_src[:, 1:])
         ws = [ws0[:]] + [ws1[:, i] for i in range(PACK - 1)]
         for i, tag in enumerate(("wsc", "xow")):
             boards.append(tile(f"board{i + 1}", [P, C], F32, tag))

@@ -58,7 +58,6 @@ def tile_list_groupboard_crossed_one_plain_kernel(
             return scales[0].bitcast(I32).rearrange("(h u r) n -> u r h n", h=2, u=2)
 
         nc.sync.dma_start(l1[:], offs)
-        nc.sync.dma_start(l3[:], offs3)
         nc.sync.dma_start(w2_raw[:], w2_words[0].rearrange("p n t -> p (n t)").bitcast(I32))
         nc.vector.memset(xo_stage[64:128], 0)
         nc.vector.memset(xt_stage[0:64], 0)
@@ -73,6 +72,7 @@ def tile_list_groupboard_crossed_one_plain_kernel(
         nc.sync.dma_start(xow[:], xo_words[0].rearrange("p n t -> p (n t)").bitcast(I32))
         nc.sync.dma_start(l2[:], offs2)
         nc.sync.dma_start(w_raw[:], w_words[0].bitcast(I32))
+        nc.sync.dma_start(l3[:], offs3)
         nc.sync.dma_start(l5[:], offs5)
         nc.sync.dma_start(l4[:], offs4)
         nc.sync.dma_start(sa_t[:], sa.rearrange("(p i) one -> p (i one)", i=PACK))
@@ -140,15 +140,15 @@ def tile_list_groupboard_crossed_one_plain_kernel(
         boards.append(tile("board3", [P, C], F32, "a_sb0"))
         nc.gpsimd.memset(boards[-1][:], 0.0)
         for i in range(1, PACK):
-            acc = ps.tile([P, J], F32, name=f"a_ps{i}")
+            acc = ps.tile([P, J], F32, name=f"a_ps{i}", tag=f"bank{i + 1}")
             product(acc[:], i, 0, slice(0, J))
             nc.scalar.copy(a_sb[i][:], acc[:])
             nc.vector.tensor_copy(boards[i][:].indirect(l3[:]), a_sb[i][:])
-        b_ps = [ps.tile([P, 2, J], F32, name=f"b_ps{i}") for i in range(PACK // 2)]
+        for i, bank in enumerate(("bank5", "bank6", "bank7", "bank0")):
+            acc = ps.tile([P, J], F32, name=f"b_ps{i}", tag=bank)
+            product(acc[:], i, 1, slice(0, J))
+            nc.scalar.copy(b_sb[i][:], acc[:])
         for i in range(PACK):
-            product(b_ps[i // 2][:, i % 2, :], i, 1, slice(0, J))
-        for i in range(PACK):
-            nc.scalar.copy(b_sb[i][:], b_ps[i // 2][:, i % 2, :])
             nc.scalar.activation(beside[:, i, :], b_sb[i][:].indirect(l5[:]), ACT.Copy)
         for i in range(PACK):
             nc.scalar.activation(picked[:, i, :], boards[i][:].indirect(l4[:]), ACT.Copy, scale=sa_t[:, i : i + 1])
@@ -166,7 +166,7 @@ def tile_list_groupboard_crossed_one_plain_kernel(
         nc.vector.quantize_mx(out=hq[:].bitcast(E4M3), scales=hs[:], in_=hid[:])
 
         for n in range(N // P):
-            y_ps = ps.tile([P, O], F32, name=f"y_ps{n}", tag=f"bank{n}")
+            y_ps = ps.tile([P, O], F32, name=f"y_ps{n}", tag=f"bank{n + 1}")
             nc.tensor.matmul_mx(out=y_ps[:], lhsT=wb_w[:, 2 * P * n : 2 * P * (n + 1)].bitcast(E2M1),
                                 lhsT_scale=wb_s[:, P * n : P * (n + 1)],
                                 rhs=hq[:].bitcast(E4M3), rhs_scale=hs[:], start=True, stop=True)

from contextlib import ExitStack

import concourse.mybir as mybir

K, T, J, R, C, O, N = 512, 1024, 256, 512, 512, 128, 256
FLOPS = 570425344

F32 = mybir.dt.float32
BF16 = mybir.dt.bfloat16
I32 = mybir.dt.int32
U32 = mybir.dt.uint32
U16 = mybir.dt.uint16
U8 = mybir.dt.uint8
E4M3 = mybir.dt.float8_e4m3fn_x4
E5M2 = mybir.dt.float8_e5m2_x4
E2M1 = mybir.dt.float4_e2m1fn_x4
ACT = mybir.ActivationFunctionType
ALU = mybir.AluOpType

P = 128
PACK = 4
H = J // 2
SPLIT = 96


def tile_list_groupboard_crossed_one_plain_kernel(
    tc, xt_words, xt_scales, xo_words, xo_scales, w_words, w_scales, w2_words, w2_scales,
    sa, wb_words, wb_scales, offs, offs2, offs3, offs4, offs5, out,
):
    nc = tc.nc
    with ExitStack() as ctx:
        sb = ctx.enter_context(tc.tile_pool(name="sb", bufs=1))
        ps = ctx.enter_context(tc.psum_pool(name="ps", bufs=1))

        def tile(name, shape, dtype, tag=""):
            return sb.tile(shape, dtype, name=name, tag=tag or name, align_bytes=64)

        l1 = tile("l1", [P, J // 16], U16)
        l2 = tile("l2", [P, J // 16], U16)
        l3 = tile("l3", [P, J // 16], U16)
        l4 = tile("l4", [P, O // 16], U16)
        l5 = tile("l5", [P, O // 16], U16)

        wsc = tile("wsc", [P, 2, 2, R // 4], I32)
        xt_stage = tile("xt_stage", [P, 2, T // 4], I32)
        xo_stage = tile("xo_stage", [P, 2, T // 4], I32)
        xts = tile("xts", [P, T], U8)
        xos = tile("xos", [P, T], U8)
        xtw = tile("xtw", [P, T], I32)
        xow = tile("xow", [P, T], I32)
        w_raw = tile("w_raw", [P, R // 2], I32)
        w2_raw = tile("w2_raw", [P, R], I32)
        wb_w = tile("wb_w", [P, 2 * N], U8)
        wb_s = tile("wb_s", [P, N], U8)
        sa_t = tile("sa_t", [P, PACK], F32)

        def quadrant_pairs(scales):
            return scales[0].bitcast(I32).rearrange("(h u r) n -> u r h n", h=2, u=2)

        nc.sync.dma_start(l1[:], offs)
        nc.sync.dma_start(w2_raw[:], w2_words[0].rearrange("p n t -> p (n t)").bitcast(I32))
        nc.vector.memset(xo_stage[64:128], 0)
        nc.vector.memset(xt_stage[0:64], 0)
        nc.vector.memset(wsc[:], 0)
        for stage, base, src in ((xo_stage, 64, xo_scales), (xt_stage, 0, xt_scales)):
            for u in range(2):
                nc.sync.dma_start(stage[base + 32 * u : base + 32 * u + 4], quadrant_pairs(src)[u])
        nc.sync.dma_start(xtw[:], xt_words[0].rearrange("p n t -> p (n t)").bitcast(I32))
        for s, src in enumerate((w_scales, w2_scales)):
            for u in range(2):
                nc.sync.dma_start(wsc[32 * u : 32 * u + 4, :, s, :], quadrant_pairs(src)[u])
        nc.sync.dma_start(xow[:], xo_words[0].rearrange("p n t -> p (n t)").bitcast(I32))
        nc.sync.dma_start(l2[:], offs2)
        nc.sync.dma_start(w_raw[:], w_words[0].bitcast(I32))
        nc.sync.dma_start(l3[:], offs3)
        nc.sync.dma_start(l5[:], offs5)
        nc.sync.dma_start(l4[:], offs4)
        nc.sync.dma_start(sa_t[:], sa.rearrange("(p i) one -> p (i one)", i=PACK))
        nc.sync.dma_start(wb_w[:].bitcast(I32), wb_words[0].bitcast(I32))

        boards = [tile("board0", [P, C], F32)]
        nc.vector.memset(boards[0][:], 0.0)
        nc.vector.memset(wb_s[:].bitcast(I32), 0)
        for q in range(4):
            nc.sync.dma_start(wb_s[32 * q : 32 * q + 4].bitcast(I32), wb_scales[0, 4 * q : 4 * q + 4].bitcast(I32))

        for plane, stage, base, order in ((xos, xo_stage, 64, (1, 0)), (xts, xt_stage, 0, (0, 1))):
            for h in order:
                nc.vector.tensor_copy(plane[64 * h : 64 * h + 64].bitcast(I32), stage[base : base + 64, h])

        xtg = tile("xtg", [P, J], U32)
        xog = tile("xog", [P, J], U32)
        xtsg = tile("xtsg", [P, J], U8)
        xosg = tile("xosg", [P, J], U8)
        nc.vector.tensor_copy(xtsg[:], xts[:].indirect(l1[:]))
        nc.vector.tensor_copy(xtg[:], xtw[:].bitcast(U32).indirect(l1[:]))

        ws0 = tile("ws0", [P, 2, P], U8)
        ws_src = wsc[:, 0].bitcast(U8).rearrange("p s (m i) -> p i s m", i=PACK)
        nc.vector.tensor_copy(wsc[64:128, 0], wsc[0:64, 1])
        nc.gpsimd.tensor_copy(ws0[:], ws_src[:, 0])

        halves = [(slice(H * h, H * (h + 1)), slice(H // 16 * h, H // 16 * (h + 1))) for h in range(2)]
        for h, (js, ls) in enumerate(halves):
            nc.vector.tensor_copy(xosg[:, js], xos[:].indirect(l2[:, ls]))
            nc.vector.tensor_copy(xog[:, js], xow[:].bitcast(U32).indirect(l2[:, ls]))
        ws1 = tile("ws1", [P, PACK - 1, 2, P], U8)
        nc.gpsimd.tensor_copy(ws1[:], ws_src[:, 1:])
        ws = [ws0[:]] + [ws1[:, i] for i in range(PACK - 1)]
        for i, tag in enumerate(("wsc", "xow")):
            boards.append(tile(f"board{i + 1}", [P, C], F32, tag))
            nc.gpsimd.memset(boards[-1][:], 0.0)

        w_p = tile("w_p", [P, PACK, 2 * P], U8)
        w2_p = tile("w2_p", [P, PACK, P], U32)
        w_src = w_raw[:].bitcast(U16).rearrange("p (m i) -> p m i", i=PACK)
        w2_src = w2_raw[:].bitcast(U32).rearrange("p (m i) -> p m i", i=PACK)
        nc.scalar.copy(w2_p[:].rearrange("p i m -> p m i"), w2_src)
        nc.scalar.copy(w_p[:, 0, :].bitcast(U16), w_src[:, :, 0])
        nc.scalar.copy(w_p[:, 1:].bitcast(U16).rearrange("p i m -> p m i"), w_src[:, :, 1:])

        def product(acc, i, first, js):
            moving = ((xtg[:, js].bitcast(E5M2), xtsg[:, js]), (xog[:, js].bitcast(E4M3), xosg[:, js]))
            for s, lhs in enumerate((w_p[:, i, :].bitcast(E2M1), w2_p[:, i, :].bitcast(E5M2))):
                rhs, rhs_scale = moving[(first + s) % 2]
                nc.tensor.matmul_mx(out=acc, lhsT=lhs, lhsT_scale=ws[i][:, s, :], rhs=rhs, rhs_scale=rhs_scale,
                                    start=(s == 0), stop=(s == 1))

        a_sb = [tile(f"a_sb{i}", [P, J], F32) for i in range(PACK)]
        b_sb = [tile(f"b_sb{i}", [P, J], F32) for i in range(PACK)]
        picked = tile("picked", [P, PACK, O], F32)
        beside = tile("beside", [P, PACK, O], F32)
        diff = tile("diff", [P, PACK, O], F32)

        for h, (js, ls) in enumerate(halves):
            acc = ps.tile([P, H], F32, name=f"a0_ps{h}", tag=f"bank{h}")
            product(acc[:], 0, 0, js)
            nc.scalar.copy(a_sb[0][:, js], acc[:])
            nc.vector.tensor_copy(boards[0][:].indirect(l3[:, ls]), a_sb[0][:, js])
        boards.append(tile("board3", [P, C], F32, "a_sb0"))
        nc.gpsimd.memset(boards[-1][:], 0.0)
        for i in range(1, PACK):
            acc = ps.tile([P, J], F32, name=f"a_ps{i}", tag=f"bank{i + 1}")
            product(acc[:], i, 0, slice(0, J))
            nc.scalar.copy(a_sb[i][:], acc[:])
            nc.vector.tensor_copy(boards[i][:].indirect(l3[:]), a_sb[i][:])
        for i, bank in enumerate(("bank5", "bank6", "bank7", "bank0")):
            acc = ps.tile([P, J], F32, name=f"b_ps{i}", tag=bank)
            product(acc[:], i, 1, slice(0, J))
            nc.scalar.copy(b_sb[i][:], acc[:])
        for i in range(PACK):
            nc.scalar.activation(beside[:, i, :], b_sb[i][:].indirect(l5[:]), ACT.Copy)
        for i in range(PACK):
            nc.scalar.activation(picked[:, i, :], boards[i][:].indirect(l4[:]), ACT.Copy, scale=sa_t[:, i : i + 1])
        nc.vector.tensor_tensor(diff[:, :3], picked[:, :3], beside[:, :3], ALU.subtract)
        nc.vector.tensor_tensor(diff[:, 3], picked[:, 3], beside[:, 3], ALU.subtract)

        hid = tile("hid", [P, O * PACK], BF16)
        hid_v = hid[:].rearrange("p (o i) -> p o i", i=PACK)
        diff_v = diff[:].rearrange("p i o -> p o i")
        nc.scalar.activation(hid[:, : PACK * SPLIT].rearrange("p (c e i) -> p c i e", e=4, i=PACK),
                             diff[:, :, :SPLIT].rearrange("p i (c e) -> p c i e", e=4), ACT.Abs)
        nc.vector.scalar_tensor_tensor(hid_v[:, SPLIT:], diff_v[:, SPLIT:], -1.0, diff_v[:, SPLIT:], ALU.mult, ALU.max)
        hq = tile("hq", [P, O], U32)
        hs = tile("hs", [P, O], U8)
        nc.vector.quantize_mx(out=hq[:].bitcast(E4M3), scales=hs[:], in_=hid[:])

        for n in range(N // P):
            y_ps = ps.tile([P, O], F32, name=f"y_ps{n}", tag=f"bank{n + 1}")
            nc.tensor.matmul_mx(out=y_ps[:], lhsT=wb_w[:, 2 * P * n : 2 * P * (n + 1)].bitcast(E2M1),
                                lhsT_scale=wb_s[:, P * n : P * (n + 1)],
                                rhs=hq[:].bitcast(E4M3), rhs_scale=hs[:], start=True, stop=True)
            y = tile(f"y{n}", [P, O], F32)
            if n == 0:
                nc.vector.tensor_copy(y[:], y_ps[:])
                nc.sync.dma_start(out[P * n : P * (n + 1), :], y[:])
            else:
                nc.scalar.copy(y[:], y_ps[:])
                nc.scalar.dma_start(out[P * n : P * (n + 1), :], y[:])
